import numpy as np
import ml_dtypes


def mxq(x, axis, fmt="e4m3"):
    dtype, down = {"e4m3": (ml_dtypes.float8_e4m3fn, 7), "e5m2": (ml_dtypes.float8_e5m2, 14)}[fmt]
    v = np.moveaxis(np.asarray(x, np.float32).astype(ml_dtypes.bfloat16).astype(np.float64), axis, -1)
    blocks = v.reshape(v.shape[:-1] + (-1, 32))
    amax = np.abs(blocks).max(-1, keepdims=True)
    byte = np.maximum(np.where(amax > 0, np.frexp(amax)[1] - 1 + 127, 0) - down, 1)
    scale = np.exp2(byte - 127.0)
    codes = (blocks / scale).astype(np.float32).astype(dtype).astype(np.float64)
    return np.moveaxis((codes * scale).reshape(v.shape), -1, axis)


WIDE = False


def mx_kscale(k):
    if not WIDE:
        return np.ones(k)
    levels = np.array([10, -10, 5, -5, 0])
    if k % 512:
        return np.exp2(np.random.permutation(np.resize(levels, k // 32))).repeat(32)
    a = np.empty((k // 512, 16))
    for p in range(k // 512):
        a[p, :8] = np.random.permutation(np.resize(levels, 8))
        for g in range(8):
            far = levels[np.abs(levels - a[p, g]) >= 10]
            a[p, g + 8] = far[np.random.randint(len(far))]
    return np.exp2(a.ravel()).repeat(32)


def f64(x):
    return np.asarray(x).astype(np.float64)


def striped(idx):
    return np.tile(np.asarray(idx).reshape(-1, 16).T, (8, 1)).astype(np.uint16)


def unstriped(offs):
    return offs[:16].T.reshape(-1).astype(np.int64)


O, G, T, D, M = 6, 256, 512, 1024, 256


def setup_inputs():
    n = np.random.standard_normal
    s = mx_kscale(D)[:, None]
    x = n((D, T)) * s
    x[:, 0] = 0.0
    idx = np.stack([np.random.permutation(T - 1)[:G] + 1 for o in range(O)])
    idx[np.random.uniform(size=(O, G)) < 0.1] = 0
    return {
        "xT": x.astype(np.float32),
        "w": (n((O, D, M)) / np.sqrt(O * D) / s).astype(np.float32),
        "bias": (0.3 * n((M, 1))).astype(np.float32),
        "offs": striped(idx.reshape(-1)),
    }


def reference(xT, w, bias, offs):
    x = f64(xT)[:, unstriped(offs)]
    wq, xq = mxq(f64(w), 1, "e4m3"), mxq(x, 0, "e4m3").reshape(D, O, G)
    y = sum(wq[o].T @ xq[:, o] for o in range(O))
    y = y + f64(bias)
    y = np.maximum(y, 0.0)
    return y

@@ -1,0 +1,167 @@
+from contextlib import ExitStack
+
+import concourse.mybir as mybir
+
+O, G, T, D, M = 6, 256, 512, 1024, 256
+FLOPS = 2 * O * G * D * M
+
+F32 = mybir.dt.float32
+BF16 = mybir.dt.bfloat16
+U32 = mybir.dt.uint32
+U16 = mybir.dt.uint16
+U8 = mybir.dt.uint8
+FP8X4 = mybir.dt.float8_e4m3fn_x4
+RELU = mybir.ActivationFunctionType.Relu
+COPY = mybir.ActivationFunctionType.Copy
+ADD, MAX, MULT = mybir.AluOpType.add, mybir.AluOpType.max, mybir.AluOpType.mult
+
+P = 128
+K_PASS = 512
+PASSES = D // K_PASS
+CHUNK = 512
+CHUNKS = O * G // CHUNK
+O_CHUNK = CHUNK // G
+VECTOR_INTERLEAVES = ((1, 2),)
+POOL_CASTS = ()
+
+
+def tile_attend_spconv_relu_kernel(tc, xT, w, bias, offs, out):
+    nc = tc.nc
+    with ExitStack() as ctx:
+        keep = ctx.enter_context(tc.tile_pool(name="keep", bufs=1))
+        psum = ctx.enter_context(tc.psum_pool(name="psum", bufs=1))
+
+        offsets = keep.tile([P, O * G // 16], U16, name="offsets")
+        xw = keep.tile([P, 5 * 2 * T], BF16, name="xw", align_bytes=64)
+        nc.vector.memset(xw[:, 4 * 2 * T :], 0.0)
+
+        x_raw = []
+        for q in range(4):
+            g, u = q // 2, q % 2
+            raw = keep.tile([P, 2, T], F32, name=f"x_raw{q}", align_bytes=64)
+            rows = xT[g * K_PASS : (g + 1) * K_PASS, :].rearrange("(p u e) c -> p u e c", u=2, e=2)
+            parts = 2 if q == 0 else 1
+            for h in range(parts):
+                cols = slice(h * T // parts, (h + 1) * T // parts)
+                nc.sync.dma_start(out=raw[:, :, cols], in_=rows[:, u, :, cols])
+            x_raw.append(raw)
+            if q == 0:
+                nc.sync.dma_start(offsets[:], offs)
+        w_raw = {}
+        for g in range(PASSES):
+            for o in range(O):
+                raw = keep.tile([P, 4, M], F32, name=f"w_raw{g}_{o}", align_bytes=64)
+                rows = w[o, g * K_PASS : (g + 1) * K_PASS, :].rearrange("(p j) m -> p j m", j=4)
+                nc.sync.dma_start(out=raw[:], in_=rows)
+                w_raw[g, o] = raw
+        bias_t = keep.tile([P, 2], F32, name="bias_t")
+        nc.sync.dma_start(out=bias_t[:], in_=bias.rearrange("(t p) o -> p (t o)", t=2))
+
+        for q in range(4):
+            dst = xw[:, (3 - q) * 2 * T : (4 - q) * 2 * T].rearrange("p (c e) -> p c e", e=2)
+            src = x_raw[q][:].rearrange("p e c -> p c e")
+            if q == 0:
+                for h in range(2):
+                    cols = slice(h * T // 2, (h + 1) * T // 2)
+                    nc.vector.tensor_copy(out=dst[:, cols, :], in_=src[:, cols, :])
+            else:
+                nc.scalar.activation(dst, src, COPY)
+
+        acc = [psum.tile([P, G], F32, name=f"acc{t}") for t in range(2)]
+        xq = {}
+        gathered = {}
+        wide = {}
+
+        def gather(g, c):
+            planes = keep.tile([P, 2, 2 * CHUNK], BF16, name=f"planes{g}_{c}", align_bytes=64)
+            for u in range(2):
+                q = 2 * g + u
+                window = xw[:, (3 - q) * 2 * T : (5 - q) * 2 * T].bitcast(U32)
+                nc.vector.tensor_copy(
+                    out=planes[:, u, :].bitcast(U32),
+                    in_=window.indirect(offsets[:, c * CHUNK // 16 : (c + 1) * CHUNK // 16]),
+                )
+            gathered[g, c] = planes
+
+        def interleave(g, c):
+            quad = keep.tile([P, 4 * CHUNK], BF16, name=f"quad{g}_{c}", align_bytes=64)
+            dst = quad[:].bitcast(F32).rearrange("p (n u) -> p n u", u=2)
+            src = gathered[g, c][:].bitcast(F32).rearrange("p u n -> p n u")
+            if (g, c) in VECTOR_INTERLEAVES:
+                nc.vector.tensor_copy(out=dst, in_=src)
+            else:
+                nc.scalar.copy(dst, src)
+            wide[g, c] = quad
+
+        def quantize_x(g, c):
+            codes = keep.tile([P, CHUNK], U32, name=f"x_codes{g}_{c}", align_bytes=64)
+            scales = keep.tile([P, CHUNK], U8, name=f"x_scales{g}_{c}", align_bytes=64)
+            nc.vector.quantize_mx(out=codes[:].bitcast(FP8X4), scales=scales[:], in_=wide[g, c][:])
+            xq[g, c] = (codes, scales)
+
+        wb = {}
+        wq = {}
+
+        def cast_w(g, c):
+            quad = keep.tile([P, O_CHUNK, M, 4], BF16, name=f"w_quad{g}_{c}", align_bytes=64)
+            for i in range(O_CHUNK):
+                if (g, c * O_CHUNK + i) in POOL_CASTS:
+                    nc.gpsimd.tensor_scalar(
+                        quad[:, i, :, :], w_raw[g, c * O_CHUNK + i][:].rearrange("p j m -> p m j"), 1.0, 0.0, MULT, ADD
+                    )
+                    continue
+                nc.scalar.copy(quad[:, i, :, :], w_raw[g, c * O_CHUNK + i][:].rearrange("p j m -> p m j"))
+            wb[g, c] = quad
+
+        def quantize_w(g, c):
+            codes = keep.tile([P, O_CHUNK * M], U32, name=f"w_codes{g}_{c}", align_bytes=64)
+            scales = keep.tile([P, O_CHUNK * M], U8, name=f"w_scales{g}_{c}", align_bytes=64)
+            parts = O_CHUNK if (g, c) == (PASSES - 1, CHUNKS - 1) else 1
+            step = O_CHUNK * M // parts
+            flat = wb[g, c][:].rearrange("p i m j -> p (i m j)")
+            for h in range(parts):
+                cols = slice(h * step, (h + 1) * step)
+                nc.vector.quantize_mx(
+                    out=codes[:, cols].bitcast(FP8X4), scales=scales[:, cols], in_=flat[:, h * step * 4 : (h + 1) * step * 4]
+                )
+            wq[g, c] = (codes, scales)
+
+        def multiply(g, c):
+            x_codes, x_scales = xq[g, c]
+            w_codes, w_scales = wq[g, c]
+            for i in range(O_CHUNK):
+                for t in range(2):
+                    m_cols = slice(i * M + t * P, i * M + (t + 1) * P)
+                    n_cols = slice(i * G, (i + 1) * G)
+                    nc.tensor.matmul_mx(
+                        out=acc[t][:],
+                        lhsT=w_codes[:, m_cols].bitcast(FP8X4),
+                        lhsT_scale=w_scales[:, m_cols],
+                        rhs=x_codes[:, n_cols].bitcast(FP8X4),
+                        rhs_scale=x_scales[:, n_cols],
+                        start=(g == 0 and c == 0 and i == 0),
+                        stop=(g == PASSES - 1 and c == CHUNKS - 1 and i == O_CHUNK - 1),
+                    )
+
+        steps = [(g, c) for g in range(PASSES) for c in range(CHUNKS)]
+        n = len(steps)
+        for k in range(n + 2):
+            if k < n:
+                gather(*steps[k])
+            if 1 <= k <= n:
+                interleave(*steps[k - 1])
+            if k < n:
+                cast_w(*steps[k])
+            if 2 <= k:
+                quantize_x(*steps[k - 2])
+                quantize_w(*steps[k - 2])
+                multiply(*steps[k - 2])
+
+        for t in range(2):
+            result = keep.tile([P, G], F32, name=f"result{t}", align_bytes=64)
+            if t == 0:
+                nc.vector.tensor_scalar(result[:], acc[t][:], bias_t[:, t : t + 1], 0.0, ADD, MAX)
+                nc.sync.dma_start(out=out[t * P : (t + 1) * P, :], in_=result[:])
+            else:
+                nc.scalar.activation(result[:], acc[t][:], RELU, bias=bias_t[:, t : t + 1])
+                nc.scalar.dma_start(out=out[t * P : (t + 1) * P, :], in_=result[:])

@@ -19,10 +19,11 @@ P = 128
 K_PASS = 512
 PASSES = D // K_PASS
 CHUNK = 512
-CHUNKS = O * G // CHUNK
-O_CHUNK = CHUNK // G
-VECTOR_INTERLEAVES = ((1, 2),)
-POOL_CASTS = ()
+X_GROUPS = (2, 2, 1, 1)
+VECTOR_INTERLEAVES = ()
+POOL_CASTS = (1, 3, 5)
+VECTOR_CASTS = ()
+LAST_SPLIT = 2
 
 
 def tile_attend_spconv_relu_kernel(tc, xT, w, bias, offs, out):
@@ -47,13 +48,13 @@ def tile_attend_spconv_relu_kernel(tc, xT, w, bias, offs, out):
             x_raw.append(raw)
             if q == 0:
                 nc.sync.dma_start(offsets[:], offs)
-        w_raw = {}
-        for g in range(PASSES):
-            for o in range(O):
-                raw = keep.tile([P, 4, M], F32, name=f"w_raw{g}_{o}", align_bytes=64)
-                rows = w[o, g * K_PASS : (g + 1) * K_PASS, :].rearrange("(p j) m -> p j m", j=4)
-                nc.sync.dma_start(out=raw[:], in_=rows)
-                w_raw[g, o] = raw
+        w_raw = []
+        for j in range(PASSES * O):
+            g, o = j // O, j % O
+            raw = keep.tile([P, 4, M], F32, name=f"w_raw{j}", align_bytes=64)
+            rows = w[o, g * K_PASS : (g + 1) * K_PASS, :].rearrange("(p j) m -> p j m", j=4)
+            nc.sync.dma_start(out=raw[:], in_=rows)
+            w_raw.append(raw)
         bias_t = keep.tile([P, 2], F32, name="bias_t")
         nc.sync.dma_start(out=bias_t[:], in_=bias.rearrange("(t p) o -> p (t o)", t=2))
 
@@ -68,94 +69,92 @@ def tile_attend_spconv_relu_kernel(tc, xT, w, bias, offs, out):
                 nc.scalar.activation(dst, src, COPY)
 
         acc = [psum.tile([P, G], F32, name=f"acc{t}") for t in range(2)]
-        xq = {}
-        gathered = {}
-        wide = {}
+        planes = {}
 
-        def gather(g, c):
-            planes = keep.tile([P, 2, 2 * CHUNK], BF16, name=f"planes{g}_{c}", align_bytes=64)
-            for u in range(2):
-                q = 2 * g + u
-                window = xw[:, (3 - q) * 2 * T : (5 - q) * 2 * T].bitcast(U32)
-                nc.vector.tensor_copy(
-                    out=planes[:, u, :].bitcast(U32),
-                    in_=window.indirect(offsets[:, c * CHUNK // 16 : (c + 1) * CHUNK // 16]),
-                )
-            gathered[g, c] = planes
+        def gather(c, u):
+            g, c3 = c // 3, c % 3
+            if u == 0:
+                planes[c] = keep.tile([P, 2, 2 * CHUNK], BF16, name=f"planes{c}", align_bytes=64)
+            q = 2 * g + u
+            window = xw[:, (3 - q) * 2 * T : (5 - q) * 2 * T].bitcast(U32)
+            nc.vector.tensor_copy(
+                out=planes[c][:, u, :].bitcast(U32),
+                in_=window.indirect(offsets[:, c3 * CHUNK // 16 : (c3 + 1) * CHUNK // 16]),
+            )
 
-        def interleave(g, c):
-            quad = keep.tile([P, 4 * CHUNK], BF16, name=f"quad{g}_{c}", align_bytes=64)
-            dst = quad[:].bitcast(F32).rearrange("p (n u) -> p n u", u=2)
-            src = gathered[g, c][:].bitcast(F32).rearrange("p u n -> p n u")
-            if (g, c) in VECTOR_INTERLEAVES:
+        def interleave(c, dst):
+            dst = dst.bitcast(F32).rearrange("p (n u) -> p n u", u=2)
+            src = planes[c][:].bitcast(F32).rearrange("p u n -> p n u")
+            if c in VECTOR_INTERLEAVES:
                 nc.vector.tensor_copy(out=dst, in_=src)
             else:
                 nc.scalar.copy(dst, src)
-            wide[g, c] = quad
 
-        def quantize_x(g, c):
-            codes = keep.tile([P, CHUNK], U32, name=f"x_codes{g}_{c}", align_bytes=64)
-            scales = keep.tile([P, CHUNK], U8, name=f"x_scales{g}_{c}", align_bytes=64)
-            nc.vector.quantize_mx(out=codes[:].bitcast(FP8X4), scales=scales[:], in_=wide[g, c][:])
-            xq[g, c] = (codes, scales)
+        def cast_w(j, dst):
+            dst = dst.rearrange("p (c i j) -> p c j i", i=4, j=4)
+            src = w_raw[j][:].rearrange("p j (c i) -> p c j i", i=4)
+            if j in POOL_CASTS:
+                nc.gpsimd.tensor_scalar(dst, src, 1.0, 0.0, MULT, ADD)
+            elif j in VECTOR_CASTS:
+                nc.vector.tensor_copy(out=dst, in_=src)
+            else:
+                nc.scalar.copy(dst, src)
 
-        wb = {}
-        wq = {}
+        def operand(name, width):
+            quad = keep.tile([P, 4 * width], BF16, name=f"{name}_quad", align_bytes=64)
+            codes = keep.tile([P, width], U32, name=f"{name}_codes", align_bytes=64)
+            scales = keep.tile([P, width], U8, name=f"{name}_scales", align_bytes=64)
+            return quad, codes, scales
 
-        def cast_w(g, c):
-            quad = keep.tile([P, O_CHUNK, M, 4], BF16, name=f"w_quad{g}_{c}", align_bytes=64)
-            for i in range(O_CHUNK):
-                if (g, c * O_CHUNK + i) in POOL_CASTS:
-                    nc.gpsimd.tensor_scalar(
-                        quad[:, i, :, :], w_raw[g, c * O_CHUNK + i][:].rearrange("p j m -> p m j"), 1.0, 0.0, MULT, ADD
-                    )
-                    continue
-                nc.scalar.copy(quad[:, i, :, :], w_raw[g, c * O_CHUNK + i][:].rearrange("p j m -> p m j"))
-            wb[g, c] = quad
+        def quantize(op, lo, hi):
+            quad, codes, scales = op
+            nc.vector.quantize_mx(
+                out=codes[:, lo:hi].bitcast(FP8X4), scales=scales[:, lo:hi], in_=quad[:, 4 * lo : 4 * hi]
+            )
 
-        def quantize_w(g, c):
-            codes = keep.tile([P, O_CHUNK * M], U32, name=f"w_codes{g}_{c}", align_bytes=64)
-            scales = keep.tile([P, O_CHUNK * M], U8, name=f"w_scales{g}_{c}", align_bytes=64)
-            parts = O_CHUNK if (g, c) == (PASSES - 1, CHUNKS - 1) else 1
-            step = O_CHUNK * M // parts
-            flat = wb[g, c][:].rearrange("p i m j -> p (i m j)")
-            for h in range(parts):
-                cols = slice(h * step, (h + 1) * step)
-                nc.vector.quantize_mx(
-                    out=codes[:, cols].bitcast(FP8X4), scales=scales[:, cols], in_=flat[:, h * step * 4 : (h + 1) * step * 4]
+        def multiply(j, x_op, x0, w_op, w0):
+            for t in range(2):
+                m_cols = slice(w0 + t * P, w0 + (t + 1) * P)
+                n_cols = slice(x0, x0 + G)
+                nc.tensor.matmul_mx(
+                    out=acc[t][:],
+                    lhsT=w_op[1][:, m_cols].bitcast(FP8X4),
+                    lhsT_scale=w_op[2][:, m_cols],
+                    rhs=x_op[1][:, n_cols].bitcast(FP8X4),
+                    rhs_scale=x_op[2][:, n_cols],
+                    start=(j == 0),
+                    stop=(j == PASSES * O - 1),
                 )
-            wq[g, c] = (codes, scales)
 
-        def multiply(g, c):
-            x_codes, x_scales = xq[g, c]
-            w_codes, w_scales = wq[g, c]
-            for i in range(O_CHUNK):
-                for t in range(2):
-                    m_cols = slice(i * M + t * P, i * M + (t + 1) * P)
-                    n_cols = slice(i * G, (i + 1) * G)
-                    nc.tensor.matmul_mx(
-                        out=acc[t][:],
-                        lhsT=w_codes[:, m_cols].bitcast(FP8X4),
-                        lhsT_scale=w_scales[:, m_cols],
-                        rhs=x_codes[:, n_cols].bitcast(FP8X4),
-                        rhs_scale=x_scales[:, n_cols],
-                        start=(g == 0 and c == 0 and i == 0),
-                        stop=(g == PASSES - 1 and c == CHUNKS - 1 and i == O_CHUNK - 1),
-                    )
-
-        steps = [(g, c) for g in range(PASSES) for c in range(CHUNKS)]
-        n = len(steps)
-        for k in range(n + 2):
-            if k < n:
-                gather(*steps[k])
-            if 1 <= k <= n:
-                interleave(*steps[k - 1])
-            if k < n:
-                cast_w(*steps[k])
-            if 2 <= k:
-                quantize_x(*steps[k - 2])
-                quantize_w(*steps[k - 2])
-                multiply(*steps[k - 2])
+        groups = []
+        first = 0
+        for size in X_GROUPS:
+            groups.append(list(range(first, first + size)))
+            first += size
+        ops = {}
+        for k in range(len(groups) + 1):
+            if k < len(groups):
+                chunks = groups[k]
+                x_op = operand(f"x{k}", len(chunks) * CHUNK)
+                w_op = operand(f"w{k}", len(chunks) * 2 * M)
+                ops[k] = (x_op, w_op)
+                for u in range(2):
+                    for c in chunks:
+                        gather(c, u)
+                for n, c in enumerate(chunks):
+                    interleave(c, x_op[0][:, n * 4 * CHUNK : (n + 1) * 4 * CHUNK])
+                for n in range(2 * len(chunks)):
+                    cast_w(2 * chunks[0] + n, w_op[0][:, n * 4 * M : (n + 1) * 4 * M])
+            if k > 0:
+                x_op, w_op = ops[k - 1]
+                chunks = groups[k - 1]
+                width = len(chunks) * CHUNK
+                quantize(x_op, 0, width)
+                parts = LAST_SPLIT if k == len(groups) else 1
+                for h in range(parts):
+                    quantize(w_op, h * width // parts, (h + 1) * width // parts)
+                for n in range(2 * len(chunks)):
+                    multiply(2 * chunks[0] + n, x_op, n * G, w_op, n * M)
 
         for t in range(2):
             result = keep.tile([P, G], F32, name=f"result{t}", align_bytes=64)

@@ -19,11 +19,11 @@ P = 128
 K_PASS = 512
 PASSES = D // K_PASS
 CHUNK = 512
-X_GROUPS = (2, 2, 1, 1)
+X_GROUPS = (1, 1, 1, 1, 1, 1)
 VECTOR_INTERLEAVES = ()
-POOL_CASTS = (1, 3, 5)
+POOL_CASTS = (1, 3, 5, 7)
 VECTOR_CASTS = ()
-LAST_SPLIT = 2
+LAST_W_WIDTHS = (256, 128, 128)
 
 
 def tile_attend_spconv_relu_kernel(tc, xT, w, bias, offs, out):
@@ -150,9 +150,10 @@ def tile_attend_spconv_relu_kernel(tc, xT, w, bias, offs, out):
                 chunks = groups[k - 1]
                 width = len(chunks) * CHUNK
                 quantize(x_op, 0, width)
-                parts = LAST_SPLIT if k == len(groups) else 1
-                for h in range(parts):
-                    quantize(w_op, h * width // parts, (h + 1) * width // parts)
+                lo = 0
+                for piece in LAST_W_WIDTHS if k == len(groups) else (width,):
+                    quantize(w_op, lo, lo + piece)
+                    lo += piece
                 for n in range(2 * len(chunks)):
                     multiply(2 * chunks[0] + n, x_op, n * G, w_op, n * M)
 

from contextlib import ExitStack

import concourse.mybir as mybir

O, G, T, D, M = 6, 256, 512, 1024, 256
FLOPS = 2 * O * G * D * M

F32 = mybir.dt.float32
BF16 = mybir.dt.bfloat16
U32 = mybir.dt.uint32
U16 = mybir.dt.uint16
U8 = mybir.dt.uint8
FP8X4 = mybir.dt.float8_e4m3fn_x4
RELU = mybir.ActivationFunctionType.Relu
COPY = mybir.ActivationFunctionType.Copy
ADD, MAX, MULT = mybir.AluOpType.add, mybir.AluOpType.max, mybir.AluOpType.mult

P = 128
K_PASS = 512
PASSES = D // K_PASS
CHUNK = 512
X_GROUPS = (1, 1, 1, 1, 1, 1)
VECTOR_INTERLEAVES = ()
POOL_CASTS = (1, 3, 5, 7)
VECTOR_CASTS = ()
LAST_W_WIDTHS = (256, 128, 128)


def tile_attend_spconv_relu_kernel(tc, xT, w, bias, offs, out):
    nc = tc.nc
    with ExitStack() as ctx:
        keep = ctx.enter_context(tc.tile_pool(name="keep", bufs=1))
        psum = ctx.enter_context(tc.psum_pool(name="psum", bufs=1))

        offsets = keep.tile([P, O * G // 16], U16, name="offsets")
        xw = keep.tile([P, 5 * 2 * T], BF16, name="xw", align_bytes=64)
        nc.vector.memset(xw[:, 4 * 2 * T :], 0.0)

        x_raw = []
        for q in range(4):
            g, u = q // 2, q % 2
            raw = keep.tile([P, 2, T], F32, name=f"x_raw{q}", align_bytes=64)
            rows = xT[g * K_PASS : (g + 1) * K_PASS, :].rearrange("(p u e) c -> p u e c", u=2, e=2)
            parts = 2 if q == 0 else 1
            for h in range(parts):
                cols = slice(h * T // parts, (h + 1) * T // parts)
                nc.sync.dma_start(out=raw[:, :, cols], in_=rows[:, u, :, cols])
            x_raw.append(raw)
            if q == 0:
                nc.sync.dma_start(offsets[:], offs)
        w_raw = []
        for j in range(PASSES * O):
            g, o = j // O, j % O
            raw = keep.tile([P, 4, M], F32, name=f"w_raw{j}", align_bytes=64)
            rows = w[o, g * K_PASS : (g + 1) * K_PASS, :].rearrange("(p j) m -> p j m", j=4)
            nc.sync.dma_start(out=raw[:], in_=rows)
            w_raw.append(raw)
        bias_t = keep.tile([P, 2], F32, name="bias_t")
        nc.sync.dma_start(out=bias_t[:], in_=bias.rearrange("(t p) o -> p (t o)", t=2))

        for q in range(4):
            dst = xw[:, (3 - q) * 2 * T : (4 - q) * 2 * T].rearrange("p (c e) -> p c e", e=2)
            src = x_raw[q][:].rearrange("p e c -> p c e")
            if q == 0:
                for h in range(2):
                    cols = slice(h * T // 2, (h + 1) * T // 2)
                    nc.vector.tensor_copy(out=dst[:, cols, :], in_=src[:, cols, :])
            else:
                nc.scalar.activation(dst, src, COPY)

        acc = [psum.tile([P, G], F32, name=f"acc{t}") for t in range(2)]
        planes = {}

        def gather(c, u):
            g, c3 = c // 3, c % 3
            if u == 0:
                planes[c] = keep.tile([P, 2, 2 * CHUNK], BF16, name=f"planes{c}", align_bytes=64)
            q = 2 * g + u
            window = xw[:, (3 - q) * 2 * T : (5 - q) * 2 * T].bitcast(U32)
            nc.vector.tensor_copy(
                out=planes[c][:, u, :].bitcast(U32),
                in_=window.indirect(offsets[:, c3 * CHUNK // 16 : (c3 + 1) * CHUNK // 16]),
            )

        def interleave(c, dst):
            dst = dst.bitcast(F32).rearrange("p (n u) -> p n u", u=2)
            src = planes[c][:].bitcast(F32).rearrange("p u n -> p n u")
            if c in VECTOR_INTERLEAVES:
                nc.vector.tensor_copy(out=dst, in_=src)
            else:
                nc.scalar.copy(dst, src)

        def cast_w(j, dst):
            dst = dst.rearrange("p (c i j) -> p c j i", i=4, j=4)
            src = w_raw[j][:].rearrange("p j (c i) -> p c j i", i=4)
            if j in POOL_CASTS:
                nc.gpsimd.tensor_scalar(dst, src, 1.0, 0.0, MULT, ADD)
            elif j in VECTOR_CASTS:
                nc.vector.tensor_copy(out=dst, in_=src)
            else:
                nc.scalar.copy(dst, src)

        def operand(name, width):
            quad = keep.tile([P, 4 * width], BF16, name=f"{name}_quad", align_bytes=64)
            codes = keep.tile([P, width], U32, name=f"{name}_codes", align_bytes=64)
            scales = keep.tile([P, width], U8, name=f"{name}_scales", align_bytes=64)
            return quad, codes, scales

        def quantize(op, lo, hi):
            quad, codes, scales = op
            nc.vector.quantize_mx(
                out=codes[:, lo:hi].bitcast(FP8X4), scales=scales[:, lo:hi], in_=quad[:, 4 * lo : 4 * hi]
            )

        def multiply(j, x_op, x0, w_op, w0):
            for t in range(2):
                m_cols = slice(w0 + t * P, w0 + (t + 1) * P)
                n_cols = slice(x0, x0 + G)
                nc.tensor.matmul_mx(
                    out=acc[t][:],
                    lhsT=w_op[1][:, m_cols].bitcast(FP8X4),
                    lhsT_scale=w_op[2][:, m_cols],
                    rhs=x_op[1][:, n_cols].bitcast(FP8X4),
                    rhs_scale=x_op[2][:, n_cols],
                    start=(j == 0),
                    stop=(j == PASSES * O - 1),
                )

        groups = []
        first = 0
        for size in X_GROUPS:
            groups.append(list(range(first, first + size)))
            first += size
        ops = {}
        for k in range(len(groups) + 1):
            if k < len(groups):
                chunks = groups[k]
                x_op = operand(f"x{k}", len(chunks) * CHUNK)
                w_op = operand(f"w{k}", len(chunks) * 2 * M)
                ops[k] = (x_op, w_op)
                for u in range(2):
                    for c in chunks:
                        gather(c, u)
                for n, c in enumerate(chunks):
                    interleave(c, x_op[0][:, n * 4 * CHUNK : (n + 1) * 4 * CHUNK])
                for n in range(2 * len(chunks)):
                    cast_w(2 * chunks[0] + n, w_op[0][:, n * 4 * M : (n + 1) * 4 * M])
            if k > 0:
                x_op, w_op = ops[k - 1]
                chunks = groups[k - 1]
                width = len(chunks) * CHUNK
                quantize(x_op, 0, width)
                lo = 0
                for piece in LAST_W_WIDTHS if k == len(groups) else (width,):
                    quantize(w_op, lo, lo + piece)
                    lo += piece
                for n in range(2 * len(chunks)):
                    multiply(2 * chunks[0] + n, x_op, n * G, w_op, n * M)

        for t in range(2):
            result = keep.tile([P, G], F32, name=f"result{t}", align_bytes=64)
            if t == 0:
                nc.vector.tensor_scalar(result[:], acc[t][:], bias_t[:, t : t + 1], 0.0, ADD, MAX)
                nc.sync.dma_start(out=out[t * P : (t + 1) * P, :], in_=result[:])
            else:
                nc.scalar.activation(result[:], acc[t][:], RELU, bias=bias_t[:, t : t + 1])
                nc.scalar.dma_start(out=out[t * P : (t + 1) * P, :], in_=result[:])
